import numpy as np
import ml_dtypes


def mxq(x, axis, fmt="e4m3"):
    dtype, down = {"e4m3": (ml_dtypes.float8_e4m3fn, 7), "e5m2": (ml_dtypes.float8_e5m2, 14)}[fmt]
    v = np.moveaxis(np.asarray(x, np.float32).astype(ml_dtypes.bfloat16).astype(np.float64), axis, -1)
    blocks = v.reshape(v.shape[:-1] + (-1, 32))
    amax = np.abs(blocks).max(-1, keepdims=True)
    byte = np.maximum(np.where(amax > 0, np.frexp(amax)[1] - 1 + 127, 0) - down, 1)
    scale = np.exp2(byte - 127.0)
    codes = (blocks / scale).astype(np.float32).astype(dtype).astype(np.float64)
    return np.moveaxis((codes * scale).reshape(v.shape), -1, axis)


WIDE = False


def mx_kscale(k):
    if not WIDE:
        return np.ones(k)
    levels = np.array([10, -10, 5, -5, 0])
    if k % 512:
        return np.exp2(np.random.permutation(np.resize(levels, k // 32))).repeat(32)
    a = np.empty((k // 512, 16))
    for p in range(k // 512):
        a[p, :8] = np.random.permutation(np.resize(levels, 8))
        for g in range(8):
            far = levels[np.abs(levels - a[p, g]) >= 10]
            a[p, g + 8] = far[np.random.randint(len(far))]
    return np.exp2(a.ravel()).repeat(32)


def f64(x):
    return np.asarray(x).astype(np.float64)


def striped(idx):
    return np.tile(idx.reshape(-1, 16).T, (8, 1)).astype(np.uint16)


def unstriped(offs):
    return offs[:16].T.reshape(-1).astype(np.int64)


def pack_weight(w):
    k, n = w.shape
    w = f64(np.asarray(w, np.float32).astype(ml_dtypes.bfloat16)).reshape(k // 32, 32, n)
    amax = np.abs(w).max(1)
    byte = np.clip(np.where(amax > 0, np.frexp(amax)[1] - 1 + 127 - 7, 1), 1, 254)
    scaled = (w * np.exp2(127.0 - byte)[:, None, :]).reshape(k, n).astype(np.float32)
    words = np.ascontiguousarray(scaled.reshape(k // 512, 128, 4, n).transpose(0, 1, 3, 2)).astype(ml_dtypes.float8_e4m3fn).view(np.uint8)
    return words, np.ascontiguousarray(byte.astype(np.uint8).reshape(k // 512, 16, n))


def unpack_weight(words, scales):
    g, p, n, _ = words.shape
    vals = np.ascontiguousarray(words).view(ml_dtypes.float8_e4m3fn).astype(np.float64) * np.repeat(np.exp2(scales.astype(np.float64) - 127.0), 8, axis=1)[..., None]
    return vals.transpose(0, 1, 3, 2).reshape(g * 512, n)


E2M1 = np.array([0.0, 0.5, 1.0, 1.5, 2.0, 3.0, 4.0, 6.0, -0.0, -0.5, -1.0, -1.5, -2.0, -3.0, -4.0, -6.0])


def pack_fp4(w):
    k, n = w.shape
    w = f64(np.asarray(w, np.float32).astype(ml_dtypes.bfloat16)).reshape(k // 32, 32, n)
    amax = np.abs(w).max(1)
    mant, ex = np.frexp(amax / 6.0)
    byte = np.clip(np.where(amax > 0, np.where(mant > 0.5, ex, ex - 1) + 127, 1), 1, 254)
    scaled = (w * np.exp2(127.0 - byte)[:, None, :]).reshape(k, n).astype(np.float32)
    c = np.ascontiguousarray(scaled.reshape(k // 512, 128, 4, n).transpose(0, 1, 3, 2)).astype(ml_dtypes.float4_e2m1fn).view(np.uint8) & 0xF
    words = (c[..., 0::2] | (c[..., 1::2] << 4)).reshape(k // 512, 128, 2 * n)
    return np.ascontiguousarray(words), np.ascontiguousarray(byte.astype(np.uint8).reshape(k // 512, 16, n))


def unpack_fp4(words, scales):
    g, _, n = scales.shape
    words = np.ascontiguousarray(words).reshape(g, 128, n, 2)
    nib = np.empty((g, 128, n, 4), np.uint8)
    nib[..., 0::2] = words & 0xF
    nib[..., 1::2] = words >> 4
    vals = E2M1[nib] * np.repeat(np.exp2(scales.astype(np.float64) - 127.0), 8, axis=1)[..., None]
    return vals.transpose(0, 1, 3, 2).reshape(g * 512, n)


def silu(v):
    return v / (1.0 + np.exp(-np.maximum(v, -700.0)))


K, T, S, D, H, N = 512, 4096, 1024, 2, 512, 256


def setup_inputs():
    n = np.random.standard_normal
    s = mx_kscale(K)[:, None]
    u = mx_kscale(H)
    packed_xT = pack_weight(n((K, T)) * s)
    packed_w2 = pack_fp4(n((H, N)) / np.sqrt(H) / u[:, None])
    return {
        "x_words": packed_xT[0],
        "x_scales": packed_xT[1],
        "w1": (n((K, H)) / np.sqrt(K) / s * u).astype(np.float32),
        "w2_words": packed_w2[0],
        "w2_scales": packed_w2[1],
        "taps": (n((H, D)) / np.sqrt(D)).astype(np.float32),
        "offs": striped(np.random.permutation(T)[:S]),
    }


def reference(x_words, x_scales, w1, w2_words, w2_scales, taps, offs):
    xq = unpack_weight(x_words, x_scales)[:, unstriped(offs)]
    h = mxq(f64(w1), 0, "e4m3").T @ xq
    z = silu(f64(taps)[:, 0:1] * h + f64(taps)[:, 1:2] * (np.pad(h, ((0, 0), (1, 0)))[:, :S]))
    return unpack_fp4(w2_words, w2_scales).T @ mxq(z, 0, "e4m3")

@@ -1,0 +1,165 @@
+from contextlib import ExitStack
+
+import concourse.mybir as mybir
+
+K, T, S, H, N = 512, 4096, 1024, 512, 256
+FLOPS = 2 * K * H * S + 2 * H * N * S
+
+F32 = mybir.dt.float32
+BF16 = mybir.dt.bfloat16
+I32 = mybir.dt.int32
+U32 = mybir.dt.uint32
+U16 = mybir.dt.uint16
+U8 = mybir.dt.uint8
+FP8X4 = mybir.dt.float8_e4m3fn_x4
+FP4X4 = mybir.dt.float4_e2m1fn_x4
+MULT = mybir.AluOpType.mult
+ADD = mybir.AluOpType.add
+COPY = mybir.ActivationFunctionType.Copy
+SILU = mybir.ActivationFunctionType.Silu
+
+P = 128
+PACK = 4
+GATHER = 512
+PAD = 4
+CHUNKS = (256, 256, 256, 128, 128)
+
+
+def tile_picked_dconv_silu_p_kernel(
+    tc, x_words, x_scales, w1, w2_words, w2_scales, taps, offs, out
+):
+    nc = tc.nc
+    with ExitStack() as ctx:
+        keep = ctx.enter_context(tc.tile_pool(name="keep", bufs=1))
+        psum_h = ctx.enter_context(tc.psum_pool(name="psum_h", bufs=6))
+        psum_o = ctx.enter_context(tc.psum_pool(name="psum_o", bufs=2))
+
+        offsets = keep.tile([P, S // 16], U16, name="offsets")
+        nc.sync.dma_start(offsets[:], offs)
+
+        xs_win = keep.tile([P, T], U8, name="xs_win", align_bytes=64)
+        nc.vector.memset(xs_win[:].bitcast(I32), 0)
+        xs_rows = x_scales[0].bitcast(I32)
+        for r in range(4):
+            nc.scalar.dma_start(out=xs_win[:].bitcast(I32)[r:P:32, :], in_=xs_rows[r:16:4, :])
+
+        w1_raw = keep.tile([P, PACK, H], F32, name="w1_raw")
+        nc.sync.dma_start(out=w1_raw[:], in_=w1.rearrange("(p j) c -> p j c", j=PACK))
+        xw_win = keep.tile([P, T], U32, name="xw_win", align_bytes=64)
+        nc.sync.dma_start(
+            out=xw_win[:].bitcast(I32), in_=x_words[0].rearrange("p n t -> p (n t)").bitcast(I32)
+        )
+
+        tap = keep.tile([P, PACK * 2], F32, name="tap")
+        nc.gpsimd.dma_start(out=tap[:], in_=taps.rearrange("(p t) d -> p (t d)", t=PACK))
+        w2_codes = keep.tile([P, 2 * N], U8, name="w2_codes", align_bytes=64)
+        nc.gpsimd.dma_start(out=w2_codes[:].bitcast(I32), in_=w2_words[0].bitcast(I32))
+
+        zero = keep.tile([P, 1], F32, name="zero")
+        nc.vector.memset(zero[:], 0.0)
+        prev = [keep.tile([P, PAD + S], F32, name="prev%d" % t) for t in range(PACK)]
+        for t in range(PACK):
+            nc.scalar.activation(prev[t][:, PAD - 1 : PAD], zero[:], SILU)
+
+        w2_plane = keep.tile([P, N], U8, name="w2_plane", align_bytes=64)
+        nc.vector.memset(w2_plane[:].bitcast(I32), 0)
+        w2_rows = w2_scales[0].bitcast(I32)
+        for r in range(4):
+            nc.gpsimd.dma_start(out=w2_plane[:].bitcast(I32)[r:P:32, :], in_=w2_rows[r:16:4, :])
+
+        x_plane = keep.tile([P, S], U8, name="x_plane", align_bytes=64)
+        nc.vector.tensor_copy(x_plane[:], xs_win[:].indirect(offsets[:]))
+
+        w1_bf = keep.tile([P, PACK * H], BF16, name="w1_bf", align_bytes=64)
+        dst = w1_bf[:].rearrange("p (t m j) -> p m t j", t=PACK, j=PACK)
+        src = w1_raw[:].rearrange("p j (m t) -> p m t j", t=PACK)
+        nc.scalar.copy(dst[:, 0:64], src[:, 0:64])
+        nc.vector.tensor_copy(dst[:, 64:128], src[:, 64:128])
+        w1_codes = keep.tile([P, H], U32, name="w1_codes", align_bytes=64)
+        w1_plane = keep.tile([P, H], U8, name="w1_plane", align_bytes=64)
+        nc.vector.quantize_mx(out=w1_codes[:].bitcast(FP8X4), scales=w1_plane[:], in_=w1_bf[:])
+
+        x_codes = []
+        for g in range(S // GATHER):
+            picked = keep.tile([P, GATHER], U32, name="x_codes%d" % g, align_bytes=64)
+            cols = slice(g * GATHER // 16, (g + 1) * GATHER // 16)
+            nc.vector.tensor_copy(picked[:], xw_win[:].indirect(offsets[:, cols]))
+            x_codes.append(picked)
+
+        starts = [sum(CHUNKS[:c]) for c in range(len(CHUNKS))]
+        out_v = out.rearrange("(a p) n -> p a n", p=P)
+        pre = {}
+        prods = {}
+
+        def first_layer(c):
+            n0, n = starts[c], CHUNKS[c]
+            g, g0 = divmod(n0, GATHER)
+            pre[c] = keep.tile([P, PACK, n], F32, name="pre%d" % c)
+            for t in range(PACK):
+                h = psum_h.tile([P, n], F32, name="h")
+                nc.tensor.matmul_mx(
+                    out=h[:],
+                    lhsT=w1_codes[:, t * P : (t + 1) * P].bitcast(FP8X4),
+                    lhsT_scale=w1_plane[:, t * P : (t + 1) * P],
+                    rhs=x_codes[g][:, g0 : g0 + n].bitcast(FP8X4),
+                    rhs_scale=x_plane[:, n0 : n0 + n],
+                    start=True,
+                    stop=True,
+                )
+                nc.scalar.activation(
+                    prev[t][:, PAD + n0 : PAD + n0 + n], h[:], COPY, scale=tap[:, 2 * t + 1 : 2 * t + 2]
+                )
+                nc.vector.scalar_tensor_tensor(
+                    pre[c][:, t, :],
+                    h[:],
+                    tap[:, 2 * t : 2 * t + 1],
+                    prev[t][:, PAD - 1 + n0 : PAD - 1 + n0 + n],
+                    MULT,
+                    ADD,
+                )
+
+        def second_layer(c):
+            n = CHUNKS[c]
+            z_bf = keep.tile([P, n, PACK], BF16, name="z_bf%d" % c, align_bytes=64)
+            nc.scalar.activation(
+                z_bf[:].rearrange("p (c i) t -> p c t i", i=4),
+                pre[c][:].rearrange("p t (c i) -> p c t i", i=4),
+                SILU,
+            )
+            z_codes = keep.tile([P, n], U32, name="z_codes%d" % c, align_bytes=64)
+            z_plane = keep.tile([P, n], U8, name="z_plane%d" % c, align_bytes=64)
+            nc.vector.quantize_mx(
+                out=z_codes[:].bitcast(FP8X4), scales=z_plane[:], in_=z_bf[:].rearrange("p n t -> p (n t)")
+            )
+            for a in range(N // P):
+                o = psum_o.tile([P, n], F32, name="o")
+                nc.tensor.matmul_mx(
+                    out=o[:],
+                    lhsT=w2_codes[:, 2 * a * P : 2 * (a + 1) * P].bitcast(FP4X4),
+                    lhsT_scale=w2_plane[:, a * P : (a + 1) * P],
+                    rhs=z_codes[:].bitcast(FP8X4),
+                    rhs_scale=z_plane[:],
+                    start=True,
+                    stop=True,
+                )
+                prods[c, a] = o
+
+        def leave(c):
+            n0, n = starts[c], CHUNKS[c]
+            res = keep.tile([P, N // P, n], F32, name="res%d" % c)
+            for a in range(N // P):
+                if c == len(CHUNKS) - 1 and a == 1:
+                    nc.scalar.copy(res[:, a, :], prods[c, a][:])
+                else:
+                    nc.vector.tensor_copy(res[:, a, :], prods[c, a][:])
+            nc.sync.dma_start(out=out_v[:, :, n0 : n0 + n], in_=res[:])
+
+        last = len(CHUNKS) - 1
+        first_layer(0)
+        for c in range(len(CHUNKS)):
+            if c < last:
+                first_layer(c + 1)
+            if c > 0:
+                leave(c - 1)
+            second_layer(c)
+        leave(last)

@@ -22,7 +22,12 @@ P = 128
 PACK = 4
 GATHER = 512
 PAD = 4
-CHUNKS = (256, 256, 256, 128, 128)
+FIRST = (256, 256, 256, 256)
+SECOND = (256, 256, 256, 128, 128)
+SHARED_FROM = 2
+SHARED_TILES = (0, 2)
+SPLIT_FROM = 0
+AHEAD = 256
 
 
 def tile_picked_dconv_silu_p_kernel(
@@ -31,29 +36,29 @@ def tile_picked_dconv_silu_p_kernel(
     nc = tc.nc
     with ExitStack() as ctx:
         keep = ctx.enter_context(tc.tile_pool(name="keep", bufs=1))
-        psum_h = ctx.enter_context(tc.psum_pool(name="psum_h", bufs=6))
-        psum_o = ctx.enter_context(tc.psum_pool(name="psum_o", bufs=2))
+        psum_h = ctx.enter_context(tc.psum_pool(name="psum_h", bufs=5))
+        psum_o = ctx.enter_context(tc.psum_pool(name="psum_o", bufs=3))
 
         offsets = keep.tile([P, S // 16], U16, name="offsets")
         nc.sync.dma_start(offsets[:], offs)
 
         xs_win = keep.tile([P, T], U8, name="xs_win", align_bytes=64)
         nc.vector.memset(xs_win[:].bitcast(I32), 0)
-        xs_rows = x_scales[0].bitcast(I32)
-        for r in range(4):
-            nc.scalar.dma_start(out=xs_win[:].bitcast(I32)[r:P:32, :], in_=xs_rows[r:16:4, :])
 
         w1_raw = keep.tile([P, PACK, H], F32, name="w1_raw")
         nc.sync.dma_start(out=w1_raw[:], in_=w1.rearrange("(p j) c -> p j c", j=PACK))
+        tap = keep.tile([P, PACK * 2], F32, name="tap")
+        nc.sync.dma_start(out=tap[:], in_=taps.rearrange("(p t) d -> p (t d)", t=PACK))
+        w2_codes = keep.tile([P, 2 * N], U8, name="w2_codes", align_bytes=64)
+        nc.sync.dma_start(out=w2_codes[:].bitcast(I32), in_=w2_words[0].bitcast(I32))
+
+        xs_rows = x_scales[0].bitcast(I32)
+        for r in range(4):
+            nc.sync.dma_start(out=xs_win[:].bitcast(I32)[r:P:32, :], in_=xs_rows[r:16:4, :])
         xw_win = keep.tile([P, T], U32, name="xw_win", align_bytes=64)
         nc.sync.dma_start(
             out=xw_win[:].bitcast(I32), in_=x_words[0].rearrange("p n t -> p (n t)").bitcast(I32)
         )
-
-        tap = keep.tile([P, PACK * 2], F32, name="tap")
-        nc.gpsimd.dma_start(out=tap[:], in_=taps.rearrange("(p t) d -> p (t d)", t=PACK))
-        w2_codes = keep.tile([P, 2 * N], U8, name="w2_codes", align_bytes=64)
-        nc.gpsimd.dma_start(out=w2_codes[:].bitcast(I32), in_=w2_words[0].bitcast(I32))
 
         zero = keep.tile([P, 1], F32, name="zero")
         nc.vector.memset(zero[:], 0.0)
@@ -65,7 +70,7 @@ def tile_picked_dconv_silu_p_kernel(
         nc.vector.memset(w2_plane[:].bitcast(I32), 0)
         w2_rows = w2_scales[0].bitcast(I32)
         for r in range(4):
-            nc.gpsimd.dma_start(out=w2_plane[:].bitcast(I32)[r:P:32, :], in_=w2_rows[r:16:4, :])
+            nc.sync.dma_start(out=w2_plane[:].bitcast(I32)[r:P:32, :], in_=w2_rows[r:16:4, :])
 
         x_plane = keep.tile([P, S], U8, name="x_plane", align_bytes=64)
         nc.vector.tensor_copy(x_plane[:], xs_win[:].indirect(offsets[:]))
@@ -86,13 +91,14 @@ def tile_picked_dconv_silu_p_kernel(
             nc.vector.tensor_copy(picked[:], xw_win[:].indirect(offsets[:, cols]))
             x_codes.append(picked)
 
-        starts = [sum(CHUNKS[:c]) for c in range(len(CHUNKS))]
+        starts1 = [sum(FIRST[:c]) for c in range(len(FIRST))]
+        starts2 = [sum(SECOND[:c]) for c in range(len(SECOND))]
         out_v = out.rearrange("(a p) n -> p a n", p=P)
         pre = {}
         prods = {}
 
         def first_layer(c):
-            n0, n = starts[c], CHUNKS[c]
+            n0, n = starts1[c], FIRST[c]
             g, g0 = divmod(n0, GATHER)
             pre[c] = keep.tile([P, PACK, n], F32, name="pre%d" % c)
             for t in range(PACK):
@@ -106,9 +112,11 @@ def tile_picked_dconv_silu_p_kernel(
                     start=True,
                     stop=True,
                 )
-                nc.scalar.activation(
-                    prev[t][:, PAD + n0 : PAD + n0 + n], h[:], COPY, scale=tap[:, 2 * t + 1 : 2 * t + 2]
-                )
+                shifted = prev[t][:, PAD + n0 : PAD + n0 + n]
+                if c >= SHARED_FROM and t in SHARED_TILES:
+                    nc.vector.tensor_scalar(shifted, h[:], tap[:, 2 * t + 1 : 2 * t + 2], None, MULT)
+                else:
+                    nc.scalar.activation(shifted, h[:], COPY, scale=tap[:, 2 * t + 1 : 2 * t + 2])
                 nc.vector.scalar_tensor_tensor(
                     pre[c][:, t, :],
                     h[:],
@@ -119,11 +127,13 @@ def tile_picked_dconv_silu_p_kernel(
                 )
 
         def second_layer(c):
-            n = CHUNKS[c]
+            n = SECOND[c]
+            f = max(k for k in range(len(FIRST)) if starts1[k] <= starts2[c])
+            f0 = starts2[c] - starts1[f]
             z_bf = keep.tile([P, n, PACK], BF16, name="z_bf%d" % c, align_bytes=64)
             nc.scalar.activation(
                 z_bf[:].rearrange("p (c i) t -> p c t i", i=4),
-                pre[c][:].rearrange("p t (c i) -> p c t i", i=4),
+                pre[f][:, :, f0 : f0 + n].rearrange("p t (c i) -> p c t i", i=4),
                 SILU,
             )
             z_codes = keep.tile([P, n], U32, name="z_codes%d" % c, align_bytes=64)
@@ -145,21 +155,22 @@ def tile_picked_dconv_silu_p_kernel(
                 prods[c, a] = o
 
         def leave(c):
-            n0, n = starts[c], CHUNKS[c]
+            n0, n = starts2[c], SECOND[c]
             res = keep.tile([P, N // P, n], F32, name="res%d" % c)
             for a in range(N // P):
-                if c == len(CHUNKS) - 1 and a == 1:
+                if c >= SPLIT_FROM and a == 1:
                     nc.scalar.copy(res[:, a, :], prods[c, a][:])
                 else:
                     nc.vector.tensor_copy(res[:, a, :], prods[c, a][:])
             nc.sync.dma_start(out=out_v[:, :, n0 : n0 + n], in_=res[:])
 
-        last = len(CHUNKS) - 1
-        first_layer(0)
-        for c in range(len(CHUNKS)):
-            if c < last:
-                first_layer(c + 1)
-            if c > 0:
+        made = 0
+        for c in range(len(SECOND)):
+            while made < len(FIRST) and starts1[made] < starts2[c] + SECOND[c] + AHEAD:
+                first_layer(made)
+                made = made + 1
+            if c >= 1:
                 leave(c - 1)
             second_layer(c)
-        leave(last)
+        for c in range(len(SECOND) - 1, len(SECOND)):
+            leave(c)

@@ -22,12 +22,12 @@ P = 128
 PACK = 4
 GATHER = 512
 PAD = 4
-FIRST = (256, 256, 256, 256)
+FIRST = (512, 512)
 SECOND = (256, 256, 256, 128, 128)
-SHARED_FROM = 2
-SHARED_TILES = (0, 2)
-SPLIT_FROM = 0
-AHEAD = 256
+SHARED_FROM = 1
+SHARED_TILES = (3,)
+SPLIT_FROM = 2
+AHEAD = 1024
 
 
 def tile_picked_dconv_silu_p_kernel(
@@ -36,29 +36,27 @@ def tile_picked_dconv_silu_p_kernel(
     nc = tc.nc
     with ExitStack() as ctx:
         keep = ctx.enter_context(tc.tile_pool(name="keep", bufs=1))
-        psum_h = ctx.enter_context(tc.psum_pool(name="psum_h", bufs=5))
-        psum_o = ctx.enter_context(tc.psum_pool(name="psum_o", bufs=3))
+        reuse = ctx.enter_context(tc.tile_pool(name="reuse", bufs=1))
+        psum_h = ctx.enter_context(tc.psum_pool(name="psum_h", bufs=4))
+        psum_o = ctx.enter_context(tc.psum_pool(name="psum_o", bufs=4))
 
         offsets = keep.tile([P, S // 16], U16, name="offsets")
         nc.sync.dma_start(offsets[:], offs)
 
-        xs_win = keep.tile([P, T], U8, name="xs_win", align_bytes=64)
+        xs_win = reuse.tile([P, T], U8, name="xs_win", align_bytes=64, offset=0)
         nc.vector.memset(xs_win[:].bitcast(I32), 0)
 
         w1_raw = keep.tile([P, PACK, H], F32, name="w1_raw")
         nc.sync.dma_start(out=w1_raw[:], in_=w1.rearrange("(p j) c -> p j c", j=PACK))
-        tap = keep.tile([P, PACK * 2], F32, name="tap")
-        nc.sync.dma_start(out=tap[:], in_=taps.rearrange("(p t) d -> p (t d)", t=PACK))
-        w2_codes = keep.tile([P, 2 * N], U8, name="w2_codes", align_bytes=64)
-        nc.sync.dma_start(out=w2_codes[:].bitcast(I32), in_=w2_words[0].bitcast(I32))
-
-        xs_rows = x_scales[0].bitcast(I32)
-        for r in range(4):
-            nc.sync.dma_start(out=xs_win[:].bitcast(I32)[r:P:32, :], in_=xs_rows[r:16:4, :])
+        nc.sync.dma_start(out=xs_win[:].bitcast(I32)[0:P:8, :], in_=x_scales[0].bitcast(I32))
         xw_win = keep.tile([P, T], U32, name="xw_win", align_bytes=64)
         nc.sync.dma_start(
             out=xw_win[:].bitcast(I32), in_=x_words[0].rearrange("p n t -> p (n t)").bitcast(I32)
         )
+        tap = keep.tile([P, PACK * 2], F32, name="tap")
+        nc.sync.dma_start(out=tap[:], in_=taps.rearrange("(p t) d -> p (t d)", t=PACK))
+        w2_codes = keep.tile([P, 2 * N], U8, name="w2_codes", align_bytes=64)
+        nc.sync.dma_start(out=w2_codes[:].bitcast(I32), in_=w2_words[0].bitcast(I32))
 
         zero = keep.tile([P, 1], F32, name="zero")
         nc.vector.memset(zero[:], 0.0)
@@ -66,23 +64,35 @@ def tile_picked_dconv_silu_p_kernel(
         for t in range(PACK):
             nc.scalar.activation(prev[t][:, PAD - 1 : PAD], zero[:], SILU)
 
-        w2_plane = keep.tile([P, N], U8, name="w2_plane", align_bytes=64)
+        x_plane = keep.tile([P, S], U8, name="x_plane", align_bytes=64)
+        nc.vector.memset(x_plane[:].bitcast(I32), 0)
+        xs_picked = keep.tile([P, S], U8, name="xs_picked", align_bytes=64)
+        nc.vector.tensor_copy(xs_picked[:], xs_win[:].indirect(offsets[:]))
+        for r in range(4):
+            nc.sync.dma_start(
+                out=x_plane[:].bitcast(I32)[r:P:32, :], in_=xs_picked[:].bitcast(I32)[8 * r : P : 32, :]
+            )
+
+        src = w1_raw[:].rearrange("p j (m t) -> p t m j", t=PACK)
+        w1_codes = reuse.tile([P, H], U32, name="w1_codes", align_bytes=64, offset=0)
+        w1_plane = keep.tile([P, H], U8, name="w1_plane", align_bytes=64)
+        for t0, t1 in ((0, 2), (2, 3), (3, 4)):
+            w1_bf = keep.tile([P, t1 - t0, P, PACK], BF16, name="w1_bf%d" % t0, align_bytes=64)
+            if t1 < PACK:
+                nc.scalar.copy(w1_bf[:], src[:, t0:t1])
+            else:
+                nc.vector.tensor_copy(w1_bf[:], src[:, t0:t1])
+            nc.vector.quantize_mx(
+                out=w1_codes[:, t0 * P : t1 * P].bitcast(FP8X4),
+                scales=w1_plane[:, t0 * P : t1 * P],
+                in_=w1_bf[:].rearrange("p t m j -> p (t m j)"),
+            )
+
+        w2_plane = reuse.tile([P, N], U8, name="w2_plane", align_bytes=64, offset=4 * H)
         nc.vector.memset(w2_plane[:].bitcast(I32), 0)
         w2_rows = w2_scales[0].bitcast(I32)
         for r in range(4):
             nc.sync.dma_start(out=w2_plane[:].bitcast(I32)[r:P:32, :], in_=w2_rows[r:16:4, :])
-
-        x_plane = keep.tile([P, S], U8, name="x_plane", align_bytes=64)
-        nc.vector.tensor_copy(x_plane[:], xs_win[:].indirect(offsets[:]))
-
-        w1_bf = keep.tile([P, PACK * H], BF16, name="w1_bf", align_bytes=64)
-        dst = w1_bf[:].rearrange("p (t m j) -> p m t j", t=PACK, j=PACK)
-        src = w1_raw[:].rearrange("p j (m t) -> p m t j", t=PACK)
-        nc.scalar.copy(dst[:, 0:64], src[:, 0:64])
-        nc.vector.tensor_copy(dst[:, 64:128], src[:, 64:128])
-        w1_codes = keep.tile([P, H], U32, name="w1_codes", align_bytes=64)
-        w1_plane = keep.tile([P, H], U8, name="w1_plane", align_bytes=64)
-        nc.vector.quantize_mx(out=w1_codes[:].bitcast(FP8X4), scales=w1_plane[:], in_=w1_bf[:])
 
         x_codes = []
         for g in range(S // GATHER):
@@ -169,8 +179,8 @@ def tile_picked_dconv_silu_p_kernel(
             while made < len(FIRST) and starts1[made] < starts2[c] + SECOND[c] + AHEAD:
                 first_layer(made)
                 made = made + 1
-            if c >= 1:
-                leave(c - 1)
+            if c >= 2:
+                leave(c - 2)
             second_layer(c)
-        for c in range(len(SECOND) - 1, len(SECOND)):
+        for c in range(len(SECOND) - 2, len(SECOND)):
             leave(c)

@@ -40,14 +40,13 @@ def tile_picked_dconv_silu_p_kernel(
         psum_h = ctx.enter_context(tc.psum_pool(name="psum_h", bufs=4))
         psum_o = ctx.enter_context(tc.psum_pool(name="psum_o", bufs=4))
 
-        offsets = keep.tile([P, S // 16], U16, name="offsets")
-        nc.sync.dma_start(offsets[:], offs)
-
         xs_win = reuse.tile([P, T], U8, name="xs_win", align_bytes=64, offset=0)
         nc.vector.memset(xs_win[:].bitcast(I32), 0)
 
         w1_raw = keep.tile([P, PACK, H], F32, name="w1_raw")
         nc.sync.dma_start(out=w1_raw[:], in_=w1.rearrange("(p j) c -> p j c", j=PACK))
+        offsets = keep.tile([P, S // 16], U16, name="offsets")
+        nc.sync.dma_start(offsets[:], offs)
         nc.sync.dma_start(out=xs_win[:].bitcast(I32)[0:P:8, :], in_=x_scales[0].bitcast(I32))
         xw_win = keep.tile([P, T], U32, name="xw_win", align_bytes=64)
         nc.sync.dma_start(
@@ -55,8 +54,6 @@ def tile_picked_dconv_silu_p_kernel(
         )
         tap = keep.tile([P, PACK * 2], F32, name="tap")
         nc.sync.dma_start(out=tap[:], in_=taps.rearrange("(p t) d -> p (t d)", t=PACK))
-        w2_codes = keep.tile([P, 2 * N], U8, name="w2_codes", align_bytes=64)
-        nc.sync.dma_start(out=w2_codes[:].bitcast(I32), in_=w2_words[0].bitcast(I32))
 
         zero = keep.tile([P, 1], F32, name="zero")
         nc.vector.memset(zero[:], 0.0)
@@ -88,6 +85,20 @@ def tile_picked_dconv_silu_p_kernel(
                 in_=w1_bf[:].rearrange("p t m j -> p (t m j)"),
             )
 
+        for i in range(3):
+            warm = psum_o.tile([P, H], F32, name="o")
+            nc.tensor.matmul_mx(
+                out=warm[:],
+                lhsT=w1_codes[:, 0:P].bitcast(FP8X4),
+                lhsT_scale=w1_plane[:, 0:P],
+                rhs=w1_codes[:].bitcast(FP8X4),
+                rhs_scale=w1_plane[:],
+                start=True,
+                stop=True,
+            )
+
+        w2_codes = reuse.tile([P, 2 * N], U8, name="w2_codes", align_bytes=64, offset=4 * H + N)
+        nc.sync.dma_start(out=w2_codes[:].bitcast(I32), in_=w2_words[0].bitcast(I32))
         w2_plane = reuse.tile([P, N], U8, name="w2_plane", align_bytes=64, offset=4 * H)
         nc.vector.memset(w2_plane[:].bitcast(I32), 0)
         w2_rows = w2_scales[0].bitcast(I32)

@@ -20,14 +20,9 @@ SILU = mybir.ActivationFunctionType.Silu
 
 P = 128
 PACK = 4
-GATHER = 512
 PAD = 4
-FIRST = (512, 512)
-SECOND = (256, 256, 256, 128, 128)
-SHARED_FROM = 1
-SHARED_TILES = (3,)
-SPLIT_FROM = 2
-AHEAD = 1024
+GATHERS = (256, 256, 512)
+STEP = 256
 
 
 def tile_picked_dconv_silu_p_kernel(
@@ -37,11 +32,11 @@ def tile_picked_dconv_silu_p_kernel(
     with ExitStack() as ctx:
         keep = ctx.enter_context(tc.tile_pool(name="keep", bufs=1))
         reuse = ctx.enter_context(tc.tile_pool(name="reuse", bufs=1))
-        psum_h = ctx.enter_context(tc.psum_pool(name="psum_h", bufs=4))
-        psum_o = ctx.enter_context(tc.psum_pool(name="psum_o", bufs=4))
+        psum = ctx.enter_context(tc.psum_pool(name="psum", bufs=1))
 
         xs_win = reuse.tile([P, T], U8, name="xs_win", align_bytes=64, offset=0)
         nc.vector.memset(xs_win[:].bitcast(I32), 0)
+
 
         w1_raw = keep.tile([P, PACK, H], F32, name="w1_raw")
         nc.sync.dma_start(out=w1_raw[:], in_=w1.rearrange("(p j) c -> p j c", j=PACK))
@@ -61,137 +56,156 @@ def tile_picked_dconv_silu_p_kernel(
         for t in range(PACK):
             nc.scalar.activation(prev[t][:, PAD - 1 : PAD], zero[:], SILU)
 
-        x_plane = keep.tile([P, S], U8, name="x_plane", align_bytes=64)
-        nc.vector.memset(x_plane[:].bitcast(I32), 0)
-        xs_picked = keep.tile([P, S], U8, name="xs_picked", align_bytes=64)
-        nc.vector.tensor_copy(xs_picked[:], xs_win[:].indirect(offsets[:]))
-        for r in range(4):
-            nc.sync.dma_start(
-                out=x_plane[:].bitcast(I32)[r:P:32, :], in_=xs_picked[:].bitcast(I32)[8 * r : P : 32, :]
+        x_planes = []
+        for half in range(2):
+            x_plane = keep.tile([P, S // 2], U8, name="x_plane%d" % half, align_bytes=64)
+            xs_picked = reuse.tile(
+                [P, S // 2], U8, name="xs_picked%d" % half, align_bytes=64, offset=T + (1 - half) * N * 3
             )
+            nc.vector.tensor_copy(xs_picked[:], xs_win[:].indirect(offsets[:, 32 * half : 32 * (half + 1)]))
+            nc.vector.tensor_copy(x_plane[:].bitcast(I32), xs_picked[:].bitcast(I32))
+            for r in range(1, 4):
+                nc.sync.dma_start(
+                    out=x_plane[:].bitcast(I32)[r:P:32, :], in_=xs_picked[:].bitcast(I32)[8 * r : P : 32, :]
+                )
+            x_planes.extend([x_plane[:, 0:STEP], x_plane[:, STEP : 2 * STEP]])
 
-        src = w1_raw[:].rearrange("p j (m t) -> p t m j", t=PACK)
-        w1_codes = reuse.tile([P, H], U32, name="w1_codes", align_bytes=64, offset=0)
+        w1_bf = keep.tile([P, PACK, P, PACK], BF16, name="w1_bf", align_bytes=64)
+        nc.scalar.copy(
+            w1_bf[:].rearrange("p t m j -> p m j t"), w1_raw[:].rearrange("p j (m t) -> p m j t", t=PACK)
+        )
+        w1_codes = keep.tile([P, H], U32, name="w1_codes", align_bytes=64)
         w1_plane = keep.tile([P, H], U8, name="w1_plane", align_bytes=64)
-        for t0, t1 in ((0, 2), (2, 3), (3, 4)):
-            w1_bf = keep.tile([P, t1 - t0, P, PACK], BF16, name="w1_bf%d" % t0, align_bytes=64)
-            if t1 < PACK:
-                nc.scalar.copy(w1_bf[:], src[:, t0:t1])
-            else:
-                nc.vector.tensor_copy(w1_bf[:], src[:, t0:t1])
-            nc.vector.quantize_mx(
-                out=w1_codes[:, t0 * P : t1 * P].bitcast(FP8X4),
-                scales=w1_plane[:, t0 * P : t1 * P],
-                in_=w1_bf[:].rearrange("p t m j -> p (t m j)"),
-            )
+        nc.vector.quantize_mx(
+            out=w1_codes[:].bitcast(FP8X4), scales=w1_plane[:], in_=w1_bf[:].rearrange("p t m j -> p (t m j)")
+        )
 
-        for i in range(3):
-            warm = psum_o.tile([P, H], F32, name="o")
-            nc.tensor.matmul_mx(
-                out=warm[:],
-                lhsT=w1_codes[:, 0:P].bitcast(FP8X4),
-                lhsT_scale=w1_plane[:, 0:P],
-                rhs=w1_codes[:].bitcast(FP8X4),
-                rhs_scale=w1_plane[:],
-                start=True,
-                stop=True,
-            )
-
-        w2_codes = reuse.tile([P, 2 * N], U8, name="w2_codes", align_bytes=64, offset=4 * H + N)
-        nc.sync.dma_start(out=w2_codes[:].bitcast(I32), in_=w2_words[0].bitcast(I32))
-        w2_plane = reuse.tile([P, N], U8, name="w2_plane", align_bytes=64, offset=4 * H)
-        nc.vector.memset(w2_plane[:].bitcast(I32), 0)
+        w2_plane = reuse.tile([P, N], U8, name="w2_plane", align_bytes=64, offset=T)
+        nc.gpsimd.memset(w2_plane[:].bitcast(I32), 0)
         w2_rows = w2_scales[0].bitcast(I32)
         for r in range(4):
             nc.sync.dma_start(out=w2_plane[:].bitcast(I32)[r:P:32, :], in_=w2_rows[r:16:4, :])
+        w2_codes = reuse.tile([P, 2 * N], U8, name="w2_codes", align_bytes=64, offset=T + N)
+        nc.sync.dma_start(out=w2_codes[:].bitcast(I32), in_=w2_words[0].bitcast(I32))
 
         x_codes = []
-        for g in range(S // GATHER):
-            picked = keep.tile([P, GATHER], U32, name="x_codes%d" % g, align_bytes=64)
-            cols = slice(g * GATHER // 16, (g + 1) * GATHER // 16)
-            nc.vector.tensor_copy(picked[:], xw_win[:].indirect(offsets[:, cols]))
-            x_codes.append(picked)
+        for g, n in enumerate(GATHERS):
+            g0 = sum(GATHERS[:g])
+            picked = keep.tile([P, n], U32, name="x_codes%d" % g, align_bytes=64)
+            nc.vector.tensor_copy(picked[:], xw_win[:].indirect(offsets[:, g0 // 16 : (g0 + n) // 16]))
+            for f0 in range(0, n, STEP):
+                x_codes.append(picked[:, f0 : f0 + STEP])
 
-        starts1 = [sum(FIRST[:c]) for c in range(len(FIRST))]
-        starts2 = [sum(SECOND[:c]) for c in range(len(SECOND))]
         out_v = out.rearrange("(a p) n -> p a n", p=P)
+        h = {}
         pre = {}
+        z_bf = {}
         prods = {}
 
-        def first_layer(c):
-            n0, n = starts1[c], FIRST[c]
-            g, g0 = divmod(n0, GATHER)
-            pre[c] = keep.tile([P, PACK, n], F32, name="pre%d" % c)
-            for t in range(PACK):
-                h = psum_h.tile([P, n], F32, name="h")
+        def products(c, ts, bank):
+            held = psum.tile([P, len(ts), STEP], F32, name="h%d_%d" % (c, ts[0]), tag="bank%d" % bank)
+            for i, t in enumerate(ts):
+                h[c, t] = held[:, i, :]
                 nc.tensor.matmul_mx(
-                    out=h[:],
+                    out=h[c, t],
                     lhsT=w1_codes[:, t * P : (t + 1) * P].bitcast(FP8X4),
                     lhsT_scale=w1_plane[:, t * P : (t + 1) * P],
-                    rhs=x_codes[g][:, g0 : g0 + n].bitcast(FP8X4),
-                    rhs_scale=x_plane[:, n0 : n0 + n],
+                    rhs=x_codes[c].bitcast(FP8X4),
+                    rhs_scale=x_planes[c],
                     start=True,
                     stop=True,
                 )
-                shifted = prev[t][:, PAD + n0 : PAD + n0 + n]
-                if c >= SHARED_FROM and t in SHARED_TILES:
-                    nc.vector.tensor_scalar(shifted, h[:], tap[:, 2 * t + 1 : 2 * t + 2], None, MULT)
-                else:
-                    nc.scalar.activation(shifted, h[:], COPY, scale=tap[:, 2 * t + 1 : 2 * t + 2])
-                nc.vector.scalar_tensor_tensor(
-                    pre[c][:, t, :],
-                    h[:],
-                    tap[:, 2 * t : 2 * t + 1],
-                    prev[t][:, PAD - 1 + n0 : PAD - 1 + n0 + n],
-                    MULT,
-                    ADD,
-                )
 
-        def second_layer(c):
-            n = SECOND[c]
-            f = max(k for k in range(len(FIRST)) if starts1[k] <= starts2[c])
-            f0 = starts2[c] - starts1[f]
-            z_bf = keep.tile([P, n, PACK], BF16, name="z_bf%d" % c, align_bytes=64)
+        def delayed(c, t, on_vector=False):
+            shifted = prev[t][:, PAD + c * STEP : PAD + (c + 1) * STEP]
+            if on_vector:
+                nc.vector.tensor_scalar(shifted, h[c, t], tap[:, 2 * t + 1 : 2 * t + 2], None, MULT)
+            else:
+                nc.scalar.activation(shifted, h[c, t], COPY, scale=tap[:, 2 * t + 1 : 2 * t + 2])
+
+        def own(c, t):
+            if c not in pre:
+                pre[c] = keep.tile([P, PACK, STEP], F32, name="pre%d" % c)
+            nc.vector.scalar_tensor_tensor(
+                pre[c][:, t, :],
+                h[c, t],
+                tap[:, 2 * t : 2 * t + 1],
+                prev[t][:, PAD - 1 + c * STEP : PAD - 1 + (c + 1) * STEP],
+                MULT,
+                ADD,
+            )
+
+        def silu(n0, n):
+            c, f0 = divmod(n0, STEP)
+            z_bf[n0] = keep.tile([P, n, PACK], BF16, name="z_bf%d" % n0, align_bytes=64)
             nc.scalar.activation(
-                z_bf[:].rearrange("p (c i) t -> p c t i", i=4),
-                pre[f][:, :, f0 : f0 + n].rearrange("p t (c i) -> p c t i", i=4),
+                z_bf[n0][:].rearrange("p (c i) t -> p c t i", i=4),
+                pre[c][:, :, f0 : f0 + n].rearrange("p t (c i) -> p c t i", i=4),
                 SILU,
             )
-            z_codes = keep.tile([P, n], U32, name="z_codes%d" % c, align_bytes=64)
-            z_plane = keep.tile([P, n], U8, name="z_plane%d" % c, align_bytes=64)
-            nc.vector.quantize_mx(
-                out=z_codes[:].bitcast(FP8X4), scales=z_plane[:], in_=z_bf[:].rearrange("p n t -> p (n t)")
-            )
-            for a in range(N // P):
-                o = psum_o.tile([P, n], F32, name="o")
-                nc.tensor.matmul_mx(
-                    out=o[:],
-                    lhsT=w2_codes[:, 2 * a * P : 2 * (a + 1) * P].bitcast(FP4X4),
-                    lhsT_scale=w2_plane[:, a * P : (a + 1) * P],
-                    rhs=z_codes[:].bitcast(FP8X4),
-                    rhs_scale=z_plane[:],
-                    start=True,
-                    stop=True,
-                )
-                prods[c, a] = o
 
-        def leave(c):
-            n0, n = starts2[c], SECOND[c]
-            res = keep.tile([P, N // P, n], F32, name="res%d" % c)
-            for a in range(N // P):
-                if c >= SPLIT_FROM and a == 1:
-                    nc.scalar.copy(res[:, a, :], prods[c, a][:])
-                else:
-                    nc.vector.tensor_copy(res[:, a, :], prods[c, a][:])
+        def second(n0, n, banks):
+            z_codes = keep.tile([P, n], U32, name="z_codes%d" % n0, align_bytes=64)
+            z_plane = keep.tile([P, n], U8, name="z_plane%d" % n0, align_bytes=64)
+            nc.vector.quantize_mx(
+                out=z_codes[:].bitcast(FP8X4), scales=z_plane[:], in_=z_bf[n0][:].rearrange("p n t -> p (n t)")
+            )
+            per_bank = (N // P) // len(banks)
+            for i, bank in enumerate(banks):
+                o = psum.tile([P, per_bank, n], F32, name="o%d_%d" % (n0, i), tag="bank%d" % bank)
+                prods[n0, i] = o
+                for a in range(i * per_bank, (i + 1) * per_bank):
+                    nc.tensor.matmul_mx(
+                        out=o[:, a - i * per_bank, :],
+                        lhsT=w2_codes[:, 2 * a * P : 2 * (a + 1) * P].bitcast(FP4X4),
+                        lhsT_scale=w2_plane[:, a * P : (a + 1) * P],
+                        rhs=z_codes[:].bitcast(FP8X4),
+                        rhs_scale=z_plane[:],
+                        start=True,
+                        stop=True,
+                    )
+
+        def leave(n0, n, copies):
+            res = keep.tile([P, N // P, n], F32, name="res%d" % n0)
+            per_bank = (N // P) // len(copies)
+            for i, copy in enumerate(copies):
+                copy(res[:, i * per_bank : (i + 1) * per_bank, :], prods[n0, i][:])
             nc.sync.dma_start(out=out_v[:, :, n0 : n0 + n], in_=res[:])
 
-        made = 0
-        for c in range(len(SECOND)):
-            while made < len(FIRST) and starts1[made] < starts2[c] + SECOND[c] + AHEAD:
-                first_layer(made)
-                made = made + 1
-            if c >= 2:
-                leave(c - 2)
-            second_layer(c)
-        for c in range(len(SECOND) - 2, len(SECOND)):
-            leave(c)
+        tiles = range(PACK)
+        for c in range(2):
+            for t in tiles:
+                products(c, (t,), PACK * c + t)
+                delayed(c, t)
+        for t in tiles:
+            own(0, t)
+        products(2, (0, 1), 0)
+        products(2, (2, 3), 1)
+        products(3, (0, 1), 2)
+        products(3, (2, 3), 3)
+        for t in tiles:
+            own(1, t)
+        silu(0, 256)
+        for t in tiles:
+            delayed(2, t)
+        second(0, 256, (4,))
+        for t in tiles:
+            own(2, t)
+        leave(0, 256, (nc.vector.tensor_copy,))
+        silu(256, 256)
+        for t in tiles:
+            delayed(3, t)
+        second(256, 256, (5,))
+        for t in tiles:
+            own(3, t)
+        for n0 in range(512, S, 128):
+            silu(n0, 128)
+        second(512, 128, (6,))
+        leave(256, 256, (nc.vector.tensor_copy,))
+        second(640, 128, (7,))
+        leave(512, 128, (nc.vector.tensor_copy,))
+        second(768, 128, (4,))
+        second(896, 128, (0, 1))
+        leave(640, 128, (nc.scalar.copy,))
+        leave(768, 128, (nc.vector.tensor_copy,))
+        leave(896, 128, (nc.scalar.copy, nc.vector.tensor_copy))

@@ -187,7 +187,7 @@ def tile_picked_dconv_silu_p_kernel(
             own(1, t)
         silu(0, 256)
         for t in tiles:
-            delayed(2, t)
+            delayed(2, t, on_vector=(t == 0))
         second(0, 256, (4,))
         for t in tiles:
             own(2, t)

@@ -42,7 +42,7 @@ def tile_picked_dconv_silu_p_kernel(
         nc.sync.dma_start(out=w1_raw[:], in_=w1.rearrange("(p j) c -> p j c", j=PACK))
         offsets = keep.tile([P, S // 16], U16, name="offsets")
         nc.sync.dma_start(offsets[:], offs)
-        nc.sync.dma_start(out=xs_win[:].bitcast(I32)[0:P:8, :], in_=x_scales[0].bitcast(I32))
+        nc.sync.dma_start(out=xs_win[:].bitcast(I32)[32:96:4, :], in_=x_scales[0].bitcast(I32))
         xw_win = keep.tile([P, T], U32, name="xw_win", align_bytes=64)
         nc.sync.dma_start(
             out=xw_win[:].bitcast(I32), in_=x_words[0].rearrange("p n t -> p (n t)").bitcast(I32)
@@ -59,14 +59,14 @@ def tile_picked_dconv_silu_p_kernel(
         x_planes = []
         for half in range(2):
             x_plane = keep.tile([P, S // 2], U8, name="x_plane%d" % half, align_bytes=64)
+            nc.vector.memset(x_plane[:].bitcast(I32), 0)
             xs_picked = reuse.tile(
-                [P, S // 2], U8, name="xs_picked%d" % half, align_bytes=64, offset=T + (1 - half) * N * 3
+                [P, S // 2], U8, name="xs_picked%d" % half, align_bytes=64, offset=T + half * N * 3
             )
             nc.vector.tensor_copy(xs_picked[:], xs_win[:].indirect(offsets[:, 32 * half : 32 * (half + 1)]))
-            nc.vector.tensor_copy(x_plane[:].bitcast(I32), xs_picked[:].bitcast(I32))
-            for r in range(1, 4):
+            for r in range(4):
                 nc.sync.dma_start(
-                    out=x_plane[:].bitcast(I32)[r:P:32, :], in_=xs_picked[:].bitcast(I32)[8 * r : P : 32, :]
+                    out=x_plane[:].bitcast(I32)[r:P:32, :], in_=xs_picked[:].bitcast(I32)[32 + 4 * r : 96 : 16, :]
                 )
             x_planes.extend([x_plane[:, 0:STEP], x_plane[:, STEP : 2 * STEP]])
 
@@ -194,7 +194,7 @@ def tile_picked_dconv_silu_p_kernel(
         leave(0, 256, (nc.vector.tensor_copy,))
         silu(256, 256)
         for t in tiles:
-            delayed(3, t)
+            delayed(3, t, on_vector=(t == 0))
         second(256, 256, (5,))
         for t in tiles:
             own(3, t)

@@ -80,12 +80,12 @@ def tile_picked_dconv_silu_p_kernel(
             out=w1_codes[:].bitcast(FP8X4), scales=w1_plane[:], in_=w1_bf[:].rearrange("p t m j -> p (t m j)")
         )
 
-        w2_plane = reuse.tile([P, N], U8, name="w2_plane", align_bytes=64, offset=T)
+        w2_plane = keep.tile([P, N], U8, name="w2_plane", align_bytes=64)
         nc.gpsimd.memset(w2_plane[:].bitcast(I32), 0)
         w2_rows = w2_scales[0].bitcast(I32)
         for r in range(4):
-            nc.sync.dma_start(out=w2_plane[:].bitcast(I32)[r:P:32, :], in_=w2_rows[r:16:4, :])
-        w2_codes = reuse.tile([P, 2 * N], U8, name="w2_codes", align_bytes=64, offset=T + N)
+            nc.gpsimd.dma_start(out=w2_plane[:].bitcast(I32)[r:P:32, :], in_=w2_rows[r:16:4, :])
+        w2_codes = reuse.tile([P, 2 * N], U8, name="w2_codes", align_bytes=64, offset=T)
         nc.sync.dma_start(out=w2_codes[:].bitcast(I32), in_=w2_words[0].bitcast(I32))
 
         x_codes = []

@@ -42,7 +42,7 @@ def tile_picked_dconv_silu_p_kernel(
         nc.sync.dma_start(out=w1_raw[:], in_=w1.rearrange("(p j) c -> p j c", j=PACK))
         offsets = keep.tile([P, S // 16], U16, name="offsets")
         nc.sync.dma_start(offsets[:], offs)
-        nc.sync.dma_start(out=xs_win[:].bitcast(I32)[32:96:4, :], in_=x_scales[0].bitcast(I32))
+        nc.sync.dma_start(out=xs_win[:].bitcast(I32)[0:P:8, :], in_=x_scales[0].bitcast(I32))
         xw_win = keep.tile([P, T], U32, name="xw_win", align_bytes=64)
         nc.sync.dma_start(
             out=xw_win[:].bitcast(I32), in_=x_words[0].rearrange("p n t -> p (n t)").bitcast(I32)
@@ -59,18 +59,16 @@ def tile_picked_dconv_silu_p_kernel(
         x_planes = []
         for half in range(2):
             x_plane = keep.tile([P, S // 2], U8, name="x_plane%d" % half, align_bytes=64)
-            nc.vector.memset(x_plane[:].bitcast(I32), 0)
-            xs_picked = reuse.tile(
-                [P, S // 2], U8, name="xs_picked%d" % half, align_bytes=64, offset=T + half * N * 3
-            )
+            xs_picked = keep.tile([P, S // 2], U8, name="xs_picked%d" % half, align_bytes=64)
             nc.vector.tensor_copy(xs_picked[:], xs_win[:].indirect(offsets[:, 32 * half : 32 * (half + 1)]))
-            for r in range(4):
+            nc.vector.tensor_copy(x_plane[:].bitcast(I32), xs_picked[:].bitcast(I32))
+            for r in range(1, 4):
                 nc.sync.dma_start(
-                    out=x_plane[:].bitcast(I32)[r:P:32, :], in_=xs_picked[:].bitcast(I32)[32 + 4 * r : 96 : 16, :]
+                    out=x_plane[:].bitcast(I32)[r:P:32, :], in_=xs_picked[:].bitcast(I32)[8 * r : P : 32, :]
                 )
             x_planes.extend([x_plane[:, 0:STEP], x_plane[:, STEP : 2 * STEP]])
 
-        w1_bf = keep.tile([P, PACK, P, PACK], BF16, name="w1_bf", align_bytes=64)
+        w1_bf = reuse.tile([P, PACK, P, PACK], BF16, name="w1_bf", align_bytes=64, offset=T)
         nc.scalar.copy(
             w1_bf[:].rearrange("p t m j -> p m j t"), w1_raw[:].rearrange("p j (m t) -> p m j t", t=PACK)
         )
@@ -80,12 +78,12 @@ def tile_picked_dconv_silu_p_kernel(
             out=w1_codes[:].bitcast(FP8X4), scales=w1_plane[:], in_=w1_bf[:].rearrange("p t m j -> p (t m j)")
         )
 
-        w2_plane = keep.tile([P, N], U8, name="w2_plane", align_bytes=64)
+        w2_plane = reuse.tile([P, N], U8, name="w2_plane", align_bytes=64, offset=T)
         nc.gpsimd.memset(w2_plane[:].bitcast(I32), 0)
         w2_rows = w2_scales[0].bitcast(I32)
         for r in range(4):
-            nc.gpsimd.dma_start(out=w2_plane[:].bitcast(I32)[r:P:32, :], in_=w2_rows[r:16:4, :])
-        w2_codes = reuse.tile([P, 2 * N], U8, name="w2_codes", align_bytes=64, offset=T)
+            nc.sync.dma_start(out=w2_plane[:].bitcast(I32)[r:P:32, :], in_=w2_rows[r:16:4, :])
+        w2_codes = reuse.tile([P, 2 * N], U8, name="w2_codes", align_bytes=64, offset=T + N)
         nc.sync.dma_start(out=w2_codes[:].bitcast(I32), in_=w2_words[0].bitcast(I32))
 
         x_codes = []
@@ -165,6 +163,12 @@ def tile_picked_dconv_silu_p_kernel(
                         stop=True,
                     )
 
+        def leave_apart(n0, n):
+            for a, (copy, queue) in enumerate(((nc.scalar.copy, nc.scalar), (nc.vector.tensor_copy, nc.sync))):
+                res = keep.tile([P, n], F32, name="res%d_%d" % (n0, a))
+                copy(res[:], prods[n0, a][:, 0, :])
+                queue.dma_start(out=out_v[:, a, n0 : n0 + n], in_=res[:])
+
         def leave(n0, n, copies):
             res = keep.tile([P, N // P, n], F32, name="res%d" % n0)
             per_bank = (N // P) // len(copies)
@@ -208,4 +212,4 @@ def tile_picked_dconv_silu_p_kernel(
         second(896, 128, (0, 1))
         leave(640, 128, (nc.scalar.copy,))
         leave(768, 128, (nc.vector.tensor_copy,))
-        leave(896, 128, (nc.scalar.copy, nc.vector.tensor_copy))
+        leave_apart(896, 128)

@@ -202,6 +202,16 @@ def tile_picked_dconv_silu_p_kernel(
         second(256, 256, (5,))
         for t in tiles:
             own(3, t)
+        warm = psum.tile([P, H], F32, name="warm", tag="bank2")
+        nc.tensor.matmul_mx(
+            out=warm[:],
+            lhsT=w1_codes[:, 0:P].bitcast(FP8X4),
+            lhsT_scale=w1_plane[:, 0:P],
+            rhs=w1_codes[:].bitcast(FP8X4),
+            rhs_scale=w1_plane[:],
+            start=True,
+            stop=True,
+        )
         for n0 in range(512, S, 128):
             silu(n0, 128)
         second(512, 128, (6,))

@@ -169,12 +169,12 @@ def tile_picked_dconv_silu_p_kernel(
                 copy(res[:], prods[n0, a][:, 0, :])
                 queue.dma_start(out=out_v[:, a, n0 : n0 + n], in_=res[:])
 
-        def leave(n0, n, copies):
+        def leave(n0, n, copies, queue=nc.sync):
             res = keep.tile([P, N // P, n], F32, name="res%d" % n0)
             per_bank = (N // P) // len(copies)
             for i, copy in enumerate(copies):
                 copy(res[:, i * per_bank : (i + 1) * per_bank, :], prods[n0, i][:])
-            nc.sync.dma_start(out=out_v[:, :, n0 : n0 + n], in_=res[:])
+            queue.dma_start(out=out_v[:, :, n0 : n0 + n], in_=res[:])
 
         tiles = range(PACK)
         for c in range(2):
@@ -220,6 +220,6 @@ def tile_picked_dconv_silu_p_kernel(
         leave(512, 128, (nc.vector.tensor_copy,))
         second(768, 128, (4,))
         second(896, 128, (0, 1))
-        leave(640, 128, (nc.scalar.copy,))
+        leave(640, 128, (nc.scalar.copy,), nc.scalar)
         leave(768, 128, (nc.vector.tensor_copy,))
         leave_apart(896, 128)

from contextlib import ExitStack

import concourse.mybir as mybir

K, T, S, H, N = 512, 4096, 1024, 512, 256
FLOPS = 2 * K * H * S + 2 * H * N * S

F32 = mybir.dt.float32
BF16 = mybir.dt.bfloat16
I32 = mybir.dt.int32
U32 = mybir.dt.uint32
U16 = mybir.dt.uint16
U8 = mybir.dt.uint8
FP8X4 = mybir.dt.float8_e4m3fn_x4
FP4X4 = mybir.dt.float4_e2m1fn_x4
MULT = mybir.AluOpType.mult
ADD = mybir.AluOpType.add
COPY = mybir.ActivationFunctionType.Copy
SILU = mybir.ActivationFunctionType.Silu

P = 128
PACK = 4
PAD = 4
GATHERS = (256, 256, 512)
STEP = 256


def tile_picked_dconv_silu_p_kernel(
    tc, x_words, x_scales, w1, w2_words, w2_scales, taps, offs, out
):
    nc = tc.nc
    with ExitStack() as ctx:
        keep = ctx.enter_context(tc.tile_pool(name="keep", bufs=1))
        reuse = ctx.enter_context(tc.tile_pool(name="reuse", bufs=1))
        psum = ctx.enter_context(tc.psum_pool(name="psum", bufs=1))

        xs_win = reuse.tile([P, T], U8, name="xs_win", align_bytes=64, offset=0)
        nc.vector.memset(xs_win[:].bitcast(I32), 0)


        w1_raw = keep.tile([P, PACK, H], F32, name="w1_raw")
        nc.sync.dma_start(out=w1_raw[:], in_=w1.rearrange("(p j) c -> p j c", j=PACK))
        offsets = keep.tile([P, S // 16], U16, name="offsets")
        nc.sync.dma_start(offsets[:], offs)
        nc.sync.dma_start(out=xs_win[:].bitcast(I32)[0:P:8, :], in_=x_scales[0].bitcast(I32))
        xw_win = keep.tile([P, T], U32, name="xw_win", align_bytes=64)
        nc.sync.dma_start(
            out=xw_win[:].bitcast(I32), in_=x_words[0].rearrange("p n t -> p (n t)").bitcast(I32)
        )
        tap = keep.tile([P, PACK * 2], F32, name="tap")
        nc.sync.dma_start(out=tap[:], in_=taps.rearrange("(p t) d -> p (t d)", t=PACK))

        zero = keep.tile([P, 1], F32, name="zero")
        nc.vector.memset(zero[:], 0.0)
        prev = [keep.tile([P, PAD + S], F32, name="prev%d" % t) for t in range(PACK)]
        for t in range(PACK):
            nc.scalar.activation(prev[t][:, PAD - 1 : PAD], zero[:], SILU)

        x_planes = []
        for half in range(2):
            x_plane = keep.tile([P, S // 2], U8, name="x_plane%d" % half, align_bytes=64)
            xs_picked = keep.tile([P, S // 2], U8, name="xs_picked%d" % half, align_bytes=64)
            nc.vector.tensor_copy(xs_picked[:], xs_win[:].indirect(offsets[:, 32 * half : 32 * (half + 1)]))
            nc.vector.tensor_copy(x_plane[:].bitcast(I32), xs_picked[:].bitcast(I32))
            for r in range(1, 4):
                nc.sync.dma_start(
                    out=x_plane[:].bitcast(I32)[r:P:32, :], in_=xs_picked[:].bitcast(I32)[8 * r : P : 32, :]
                )
            x_planes.extend([x_plane[:, 0:STEP], x_plane[:, STEP : 2 * STEP]])

        w1_bf = reuse.tile([P, PACK, P, PACK], BF16, name="w1_bf", align_bytes=64, offset=T)
        nc.scalar.copy(
            w1_bf[:].rearrange("p t m j -> p m j t"), w1_raw[:].rearrange("p j (m t) -> p m j t", t=PACK)
        )
        w1_codes = keep.tile([P, H], U32, name="w1_codes", align_bytes=64)
        w1_plane = keep.tile([P, H], U8, name="w1_plane", align_bytes=64)
        nc.vector.quantize_mx(
            out=w1_codes[:].bitcast(FP8X4), scales=w1_plane[:], in_=w1_bf[:].rearrange("p t m j -> p (t m j)")
        )

        w2_plane = reuse.tile([P, N], U8, name="w2_plane", align_bytes=64, offset=T)
        nc.gpsimd.memset(w2_plane[:].bitcast(I32), 0)
        w2_rows = w2_scales[0].bitcast(I32)
        for r in range(4):
            nc.sync.dma_start(out=w2_plane[:].bitcast(I32)[r:P:32, :], in_=w2_rows[r:16:4, :])
        w2_codes = reuse.tile([P, 2 * N], U8, name="w2_codes", align_bytes=64, offset=T + N)
        nc.sync.dma_start(out=w2_codes[:].bitcast(I32), in_=w2_words[0].bitcast(I32))

        x_codes = []
        for g, n in enumerate(GATHERS):
            g0 = sum(GATHERS[:g])
            picked = keep.tile([P, n], U32, name="x_codes%d" % g, align_bytes=64)
            nc.vector.tensor_copy(picked[:], xw_win[:].indirect(offsets[:, g0 // 16 : (g0 + n) // 16]))
            for f0 in range(0, n, STEP):
                x_codes.append(picked[:, f0 : f0 + STEP])

        out_v = out.rearrange("(a p) n -> p a n", p=P)
        h = {}
        pre = {}
        z_bf = {}
        prods = {}

        def products(c, ts, bank):
            held = psum.tile([P, len(ts), STEP], F32, name="h%d_%d" % (c, ts[0]), tag="bank%d" % bank)
            for i, t in enumerate(ts):
                h[c, t] = held[:, i, :]
                nc.tensor.matmul_mx(
                    out=h[c, t],
                    lhsT=w1_codes[:, t * P : (t + 1) * P].bitcast(FP8X4),
                    lhsT_scale=w1_plane[:, t * P : (t + 1) * P],
                    rhs=x_codes[c].bitcast(FP8X4),
                    rhs_scale=x_planes[c],
                    start=True,
                    stop=True,
                )

        def delayed(c, t, on_vector=False):
            shifted = prev[t][:, PAD + c * STEP : PAD + (c + 1) * STEP]
            if on_vector:
                nc.vector.tensor_scalar(shifted, h[c, t], tap[:, 2 * t + 1 : 2 * t + 2], None, MULT)
            else:
                nc.scalar.activation(shifted, h[c, t], COPY, scale=tap[:, 2 * t + 1 : 2 * t + 2])

        def own(c, t):
            if c not in pre:
                pre[c] = keep.tile([P, PACK, STEP], F32, name="pre%d" % c)
            nc.vector.scalar_tensor_tensor(
                pre[c][:, t, :],
                h[c, t],
                tap[:, 2 * t : 2 * t + 1],
                prev[t][:, PAD - 1 + c * STEP : PAD - 1 + (c + 1) * STEP],
                MULT,
                ADD,
            )

        def silu(n0, n):
            c, f0 = divmod(n0, STEP)
            z_bf[n0] = keep.tile([P, n, PACK], BF16, name="z_bf%d" % n0, align_bytes=64)
            nc.scalar.activation(
                z_bf[n0][:].rearrange("p (c i) t -> p c t i", i=4),
                pre[c][:, :, f0 : f0 + n].rearrange("p t (c i) -> p c t i", i=4),
                SILU,
            )

        def second(n0, n, banks):
            z_codes = keep.tile([P, n], U32, name="z_codes%d" % n0, align_bytes=64)
            z_plane = keep.tile([P, n], U8, name="z_plane%d" % n0, align_bytes=64)
            nc.vector.quantize_mx(
                out=z_codes[:].bitcast(FP8X4), scales=z_plane[:], in_=z_bf[n0][:].rearrange("p n t -> p (n t)")
            )
            per_bank = (N // P) // len(banks)
            for i, bank in enumerate(banks):
                o = psum.tile([P, per_bank, n], F32, name="o%d_%d" % (n0, i), tag="bank%d" % bank)
                prods[n0, i] = o
                for a in range(i * per_bank, (i + 1) * per_bank):
                    nc.tensor.matmul_mx(
                        out=o[:, a - i * per_bank, :],
                        lhsT=w2_codes[:, 2 * a * P : 2 * (a + 1) * P].bitcast(FP4X4),
                        lhsT_scale=w2_plane[:, a * P : (a + 1) * P],
                        rhs=z_codes[:].bitcast(FP8X4),
                        rhs_scale=z_plane[:],
                        start=True,
                        stop=True,
                    )

        def leave_apart(n0, n):
            for a, (copy, queue) in enumerate(((nc.scalar.copy, nc.scalar), (nc.vector.tensor_copy, nc.sync))):
                res = keep.tile([P, n], F32, name="res%d_%d" % (n0, a))
                copy(res[:], prods[n0, a][:, 0, :])
                queue.dma_start(out=out_v[:, a, n0 : n0 + n], in_=res[:])

        def leave(n0, n, copies, queue=nc.sync):
            res = keep.tile([P, N // P, n], F32, name="res%d" % n0)
            per_bank = (N // P) // len(copies)
            for i, copy in enumerate(copies):
                copy(res[:, i * per_bank : (i + 1) * per_bank, :], prods[n0, i][:])
            queue.dma_start(out=out_v[:, :, n0 : n0 + n], in_=res[:])

        tiles = range(PACK)
        for c in range(2):
            for t in tiles:
                products(c, (t,), PACK * c + t)
                delayed(c, t)
        for t in tiles:
            own(0, t)
        products(2, (0, 1), 0)
        products(2, (2, 3), 1)
        products(3, (0, 1), 2)
        products(3, (2, 3), 3)
        for t in tiles:
            own(1, t)
        silu(0, 256)
        for t in tiles:
            delayed(2, t, on_vector=(t == 0))
        second(0, 256, (4,))
        for t in tiles:
            own(2, t)
        leave(0, 256, (nc.vector.tensor_copy,))
        silu(256, 256)
        for t in tiles:
            delayed(3, t, on_vector=(t == 0))
        second(256, 256, (5,))
        for t in tiles:
            own(3, t)
        warm = psum.tile([P, H], F32, name="warm", tag="bank2")
        nc.tensor.matmul_mx(
            out=warm[:],
            lhsT=w1_codes[:, 0:P].bitcast(FP8X4),
            lhsT_scale=w1_plane[:, 0:P],
            rhs=w1_codes[:].bitcast(FP8X4),
            rhs_scale=w1_plane[:],
            start=True,
            stop=True,
        )
        for n0 in range(512, S, 128):
            silu(n0, 128)
        second(512, 128, (6,))
        leave(256, 256, (nc.vector.tensor_copy,))
        second(640, 128, (7,))
        leave(512, 128, (nc.vector.tensor_copy,))
        second(768, 128, (4,))
        second(896, 128, (0, 1))
        leave(640, 128, (nc.scalar.copy,), nc.scalar)
        leave(768, 128, (nc.vector.tensor_copy,))
        leave_apart(896, 128)
